import numpy as np
import ml_dtypes

BF16 = ml_dtypes.bfloat16


def bf(x):
    return np.asarray(x, np.float32).astype(BF16)


def f32(x):
    return np.asarray(x, np.float32)


def f64(x):
    return np.asarray(x).astype(np.float64)


def striped(idx):
    return np.tile(idx.reshape(-1, 16).T, (8, 1))


def rows(idx, k):
    return np.tile(idx, (k, 1))


def look(tab, idx):
    return np.take_along_axis(f64(tab), rows(idx, len(tab)), axis=1)


K, S, V, N, M = 512, 2048, 512, 512, 512


def setup_inputs():
    return {"tab": f32(np.random.standard_normal((K, S))), "y": f32(np.random.standard_normal((K, V))), "w": bf(np.random.standard_normal((K, M)) / np.sqrt(K)), "offs": striped(np.random.permutation(S)[:N])}


def reference(tab, y, w, offs):
    idx = offs[:16].T.reshape(-1)
    t = look(tab, idx)
    x = t**2 * f64(y)
    y = f64(w).T @ x
    return y

@@ -1,0 +1,62 @@
+import concourse.mybir as mybir
+
+P = 128
+ROWS, TABLE_COLS, PICKS, OUT_ROWS = 512, 2048, 512, 512
+ROW_BLOCKS = ROWS // P
+OUT_BLOCKS = OUT_ROWS // P
+HALF = ROW_BLOCKS // 2
+
+FLOPS = 2 * ROWS * OUT_ROWS * PICKS
+
+F32, BF16, U16 = mybir.dt.float32, mybir.dt.bfloat16, mybir.dt.uint16
+SQUARE = mybir.ActivationFunctionType.Square
+MULT = mybir.AluOpType.mult
+
+
+def tile_lookup_gate_sq_none_kernel(tc, tab, y, w, offs, out):
+    nc = tc.nc
+    tab_rows = tab.rearrange("(p k) s -> p k s", k=ROW_BLOCKS)
+    y_rows = y.rearrange("(p k) j -> p k j", k=ROW_BLOCKS)
+    w_rows = w.rearrange("(p k) m -> p k m", k=ROW_BLOCKS)
+
+    with (
+        tc.tile_pool(name="held", bufs=1) as held,
+        tc.psum_pool(name="psum", bufs=1) as psum,
+    ):
+        offsets = held.tile([P, PICKS // 16], U16, name="offsets")
+        windows = [held.tile([P, TABLE_COLS], F32, name=f"window{k}") for k in range(ROW_BLOCKS)]
+        squares = [held.tile([P, PICKS], F32, name=f"squares{k}") for k in range(ROW_BLOCKS)]
+        gated = [held.tile([P, PICKS], BF16, name=f"gated{k}") for k in range(ROW_BLOCKS)]
+        y_early = held.tile([P, HALF, PICKS], F32, name="y_early")
+        y_late = [held.tile([P, PICKS], F32, name=f"y_late{k}") for k in range(HALF)]
+        w_early = held.tile([P, HALF, OUT_ROWS], BF16, name="w_early")
+        w_late = held.tile([P, HALF, OUT_ROWS], BF16, name="w_late")
+        sums = [psum.tile([P, PICKS], F32, name=f"sums{b}") for b in range(OUT_BLOCKS)]
+        staged = [held.tile([P, PICKS], F32, name=f"staged{b}") for b in range(OUT_BLOCKS)]
+
+        nc.sync.dma_start(windows[0][:], tab_rows[:, 0, :])
+        nc.sync.dma_start(offsets[:], offs)
+        for k in range(1, ROW_BLOCKS - 1):
+            nc.sync.dma_start(windows[k][:], tab_rows[:, k, :])
+        nc.sync.dma_start(w_early[:], w_rows[:, :HALF, :])
+        nc.sync.dma_start(y_early[:], y_rows[:, :HALF, :])
+        nc.sync.dma_start(windows[-1][:], tab_rows[:, ROW_BLOCKS - 1, :])
+        nc.sync.dma_start(y_late[0][:], y_rows[:, HALF, :])
+        nc.sync.dma_start(w_late[:], w_rows[:, HALF:, :])
+        nc.sync.dma_start(y_late[1][:], y_rows[:, HALF + 1, :])
+
+        streams = [y_early[:, k, :] for k in range(HALF)] + [t[:] for t in y_late]
+        for k in range(ROW_BLOCKS):
+            weights = w_early[:, k, :] if k < HALF else w_late[:, k - HALF, :]
+            nc.scalar.activation(squares[k][:], windows[k][:].indirect(offsets[:]), SQUARE)
+            nc.vector.tensor_tensor(gated[k][:], squares[k][:], streams[k], MULT)
+            for b in range(OUT_BLOCKS):
+                nc.tensor.matmul(sums[b][:], weights[:, b * P:(b + 1) * P], gated[k][:],
+                                 start=(k == 0), stop=(k == ROW_BLOCKS - 1))
+
+        for b in range(OUT_BLOCKS):
+            if b % 2 == 0:
+                nc.scalar.copy(staged[b][:], sums[b][:])
+            else:
+                nc.vector.tensor_copy(staged[b][:], sums[b][:])
+            nc.sync.dma_start(out[b * P:(b + 1) * P, :], staged[b][:])

@@ -4,7 +4,10 @@ P = 128
 ROWS, TABLE_COLS, PICKS, OUT_ROWS = 512, 2048, 512, 512
 ROW_BLOCKS = ROWS // P
 OUT_BLOCKS = OUT_ROWS // P
-HALF = ROW_BLOCKS // 2
+EARLY = ROW_BLOCKS // 2
+PIECES = 2
+PIECE = PICKS // PIECES
+WARM_UPS = EARLY * OUT_BLOCKS * PIECES
 
 FLOPS = 2 * ROWS * OUT_ROWS * PICKS
 
@@ -27,36 +30,55 @@ def tile_lookup_gate_sq_none_kernel(tc, tab, y, w, offs, out):
         windows = [held.tile([P, TABLE_COLS], F32, name=f"window{k}") for k in range(ROW_BLOCKS)]
         squares = [held.tile([P, PICKS], F32, name=f"squares{k}") for k in range(ROW_BLOCKS)]
         gated = [held.tile([P, PICKS], BF16, name=f"gated{k}") for k in range(ROW_BLOCKS)]
-        y_early = held.tile([P, HALF, PICKS], F32, name="y_early")
-        y_late = [held.tile([P, PICKS], F32, name=f"y_late{k}") for k in range(HALF)]
-        w_early = held.tile([P, HALF, OUT_ROWS], BF16, name="w_early")
-        w_late = held.tile([P, HALF, OUT_ROWS], BF16, name="w_late")
-        sums = [psum.tile([P, PICKS], F32, name=f"sums{b}") for b in range(OUT_BLOCKS)]
+        y_early = held.tile([P, EARLY, PICKS], F32, name="y_early")
+        y_late = [held.tile([P, PICKS], F32, name=f"y_late{k}") for k in range(EARLY, ROW_BLOCKS)]
+        w_early = held.tile([P, EARLY, OUT_ROWS], BF16, name="w_early")
+        w_late = held.tile([P, ROW_BLOCKS - EARLY, OUT_ROWS], BF16, name="w_late")
+        sums = [[psum.tile([P, PIECE], F32, name=f"sums{b}_{h}") for h in range(PIECES)]
+                for b in range(OUT_BLOCKS)]
         staged = [held.tile([P, PICKS], F32, name=f"staged{b}") for b in range(OUT_BLOCKS)]
 
         nc.sync.dma_start(windows[0][:], tab_rows[:, 0, :])
         nc.sync.dma_start(offsets[:], offs)
-        for k in range(1, ROW_BLOCKS - 1):
-            nc.sync.dma_start(windows[k][:], tab_rows[:, k, :])
-        nc.sync.dma_start(w_early[:], w_rows[:, :HALF, :])
-        nc.sync.dma_start(y_early[:], y_rows[:, :HALF, :])
-        nc.sync.dma_start(windows[-1][:], tab_rows[:, ROW_BLOCKS - 1, :])
-        nc.sync.dma_start(y_late[0][:], y_rows[:, HALF, :])
-        nc.sync.dma_start(w_late[:], w_rows[:, HALF:, :])
-        nc.sync.dma_start(y_late[1][:], y_rows[:, HALF + 1, :])
+        nc.sync.dma_start(windows[1][:], tab_rows[:, 1, :])
+        nc.sync.dma_start(w_early[:], w_rows[:, :EARLY, :])
+        nc.sync.dma_start(windows[2][:], tab_rows[:, 2, :])
+        nc.sync.dma_start(y_early[:], y_rows[:, :EARLY, :])
+        nc.sync.dma_start(windows[3][:], tab_rows[:, 3, :])
+        for k in range(EARLY, ROW_BLOCKS):
+            nc.sync.dma_start(y_late[k - EARLY][:], y_rows[:, k, :])
+        nc.sync.dma_start(w_late[:], w_rows[:, EARLY:, :])
 
-        streams = [y_early[:, k, :] for k in range(HALF)] + [t[:] for t in y_late]
+        streams = [y_early[:, k, :] for k in range(EARLY)] + [t[:] for t in y_late]
+        weights = [w_early[:, k, :] for k in range(EARLY)]
+        weights += [w_late[:, k, :] for k in range(ROW_BLOCKS - EARLY)]
+        pieces = [slice(h * PIECE, (h + 1) * PIECE) for h in range(PIECES)]
+
+        for n in range(WARM_UPS):
+            nc.tensor.matmul(sums[0][0][:], weights[0][:, :P], weights[0][:, :PIECE],
+                             start=True, stop=True)
+
         for k in range(ROW_BLOCKS):
-            weights = w_early[:, k, :] if k < HALF else w_late[:, k - HALF, :]
-            nc.scalar.activation(squares[k][:], windows[k][:].indirect(offsets[:]), SQUARE)
-            nc.vector.tensor_tensor(gated[k][:], squares[k][:], streams[k], MULT)
-            for b in range(OUT_BLOCKS):
-                nc.tensor.matmul(sums[b][:], weights[:, b * P:(b + 1) * P], gated[k][:],
-                                 start=(k == 0), stop=(k == ROW_BLOCKS - 1))
+            for h, cols in enumerate(pieces):
+                entries = offsets[:, h * PIECE // 16:(h + 1) * PIECE // 16]
+                nc.scalar.activation(squares[k][:, cols], windows[k][:].indirect(entries), SQUARE)
+                nc.vector.tensor_tensor(gated[k][:, cols], squares[k][:, cols],
+                                        streams[k][:, cols], MULT)
+
+        def accumulate(k, b, h):
+            nc.tensor.matmul(sums[b][h][:], weights[k][:, b * P:(b + 1) * P],
+                             gated[k][:, pieces[h]],
+                             start=(k == 0), stop=(k == ROW_BLOCKS - 1))
+
+        for k in range(EARLY):
+            for h in range(PIECES):
+                for b in range(OUT_BLOCKS):
+                    accumulate(k, b, h)
 
         for b in range(OUT_BLOCKS):
-            if b % 2 == 0:
-                nc.scalar.copy(staged[b][:], sums[b][:])
-            else:
-                nc.vector.tensor_copy(staged[b][:], sums[b][:])
+            for h in range(PIECES):
+                for k in range(EARLY, ROW_BLOCKS):
+                    accumulate(k, b, h)
+            nc.scalar.copy(staged[b][:, pieces[0]], sums[b][0][:])
+            nc.vector.tensor_copy(staged[b][:, pieces[1]], sums[b][1][:])
             nc.sync.dma_start(out[b * P:(b + 1) * P, :], staged[b][:])

@@ -5,6 +5,7 @@ ROWS, TABLE_COLS, PICKS, OUT_ROWS = 512, 2048, 512, 512
 ROW_BLOCKS = ROWS // P
 OUT_BLOCKS = OUT_ROWS // P
 EARLY = ROW_BLOCKS // 2
+LATE = ROW_BLOCKS - EARLY
 PIECES = 2
 PIECE = PICKS // PIECES
 WARM_UPS = EARLY * OUT_BLOCKS * PIECES
@@ -31,12 +32,14 @@ def tile_lookup_gate_sq_none_kernel(tc, tab, y, w, offs, out):
         squares = [held.tile([P, PICKS], F32, name=f"squares{k}") for k in range(ROW_BLOCKS)]
         gated = [held.tile([P, PICKS], BF16, name=f"gated{k}") for k in range(ROW_BLOCKS)]
         y_early = held.tile([P, EARLY, PICKS], F32, name="y_early")
-        y_late = [held.tile([P, PICKS], F32, name=f"y_late{k}") for k in range(EARLY, ROW_BLOCKS)]
+        y_late = [held.tile([P, LATE, PIECE], F32, name=f"y_late{h}") for h in range(PIECES)]
         w_early = held.tile([P, EARLY, OUT_ROWS], BF16, name="w_early")
-        w_late = held.tile([P, ROW_BLOCKS - EARLY, OUT_ROWS], BF16, name="w_late")
+        w_late = held.tile([P, LATE, OUT_ROWS], BF16, name="w_late")
         sums = [[psum.tile([P, PIECE], F32, name=f"sums{b}_{h}") for h in range(PIECES)]
                 for b in range(OUT_BLOCKS)]
-        staged = [held.tile([P, PICKS], F32, name=f"staged{b}") for b in range(OUT_BLOCKS)]
+        staged = [[held.tile([P, PIECE], F32, name=f"staged{b}_{h}") for h in range(PIECES)]
+                  for b in range(OUT_BLOCKS)]
+        pieces = [slice(h * PIECE, (h + 1) * PIECE) for h in range(PIECES)]
 
         nc.sync.dma_start(windows[0][:], tab_rows[:, 0, :])
         nc.sync.dma_start(offsets[:], offs)
@@ -45,40 +48,45 @@ def tile_lookup_gate_sq_none_kernel(tc, tab, y, w, offs, out):
         nc.sync.dma_start(windows[2][:], tab_rows[:, 2, :])
         nc.sync.dma_start(y_early[:], y_rows[:, :EARLY, :])
         nc.sync.dma_start(windows[3][:], tab_rows[:, 3, :])
-        for k in range(EARLY, ROW_BLOCKS):
-            nc.sync.dma_start(y_late[k - EARLY][:], y_rows[:, k, :])
+        nc.sync.dma_start(y_late[0][:], y_rows[:, EARLY:, pieces[0]])
         nc.sync.dma_start(w_late[:], w_rows[:, EARLY:, :])
+        nc.sync.dma_start(y_late[1][:], y_rows[:, EARLY:, pieces[1]])
 
-        streams = [y_early[:, k, :] for k in range(EARLY)] + [t[:] for t in y_late]
         weights = [w_early[:, k, :] for k in range(EARLY)]
-        weights += [w_late[:, k, :] for k in range(ROW_BLOCKS - EARLY)]
-        pieces = [slice(h * PIECE, (h + 1) * PIECE) for h in range(PIECES)]
+        weights += [w_late[:, k, :] for k in range(LATE)]
 
         for n in range(WARM_UPS):
             nc.tensor.matmul(sums[0][0][:], weights[0][:, :P], weights[0][:, :PIECE],
                              start=True, stop=True)
 
-        for k in range(ROW_BLOCKS):
-            for h, cols in enumerate(pieces):
-                entries = offsets[:, h * PIECE // 16:(h + 1) * PIECE // 16]
-                nc.scalar.activation(squares[k][:, cols], windows[k][:].indirect(entries), SQUARE)
-                nc.vector.tensor_tensor(gated[k][:, cols], squares[k][:, cols],
-                                        streams[k][:, cols], MULT)
+        def look_up(k, h):
+            entries = offsets[:, h * PIECE // 16:(h + 1) * PIECE // 16]
+            nc.scalar.activation(squares[k][:, pieces[h]], windows[k][:].indirect(entries), SQUARE)
+
+        def gate(k, h, stream):
+            nc.vector.tensor_tensor(gated[k][:, pieces[h]], squares[k][:, pieces[h]], stream, MULT)
 
         def accumulate(k, b, h):
             nc.tensor.matmul(sums[b][h][:], weights[k][:, b * P:(b + 1) * P],
                              gated[k][:, pieces[h]],
                              start=(k == 0), stop=(k == ROW_BLOCKS - 1))
 
+        for k in range(ROW_BLOCKS):
+            for h in range(PIECES):
+                look_up(k, h)
+
         for k in range(EARLY):
             for h in range(PIECES):
+                gate(k, h, y_early[:, k, pieces[h]])
                 for b in range(OUT_BLOCKS):
                     accumulate(k, b, h)
 
-        for b in range(OUT_BLOCKS):
-            for h in range(PIECES):
+        copies = [nc.scalar.copy, nc.vector.tensor_copy]
+        for h in range(PIECES):
+            for k in range(EARLY, ROW_BLOCKS):
+                gate(k, h, y_late[h][:, k - EARLY, :])
+            for b in range(OUT_BLOCKS):
                 for k in range(EARLY, ROW_BLOCKS):
                     accumulate(k, b, h)
-            nc.scalar.copy(staged[b][:, pieces[0]], sums[b][0][:])
-            nc.vector.tensor_copy(staged[b][:, pieces[1]], sums[b][1][:])
-            nc.sync.dma_start(out[b * P:(b + 1) * P, :], staged[b][:])
+                copies[h](staged[b][h][:], sums[b][h][:])
+                nc.sync.dma_start(out[b * P:(b + 1) * P, pieces[h]], staged[b][h][:])

import concourse.mybir as mybir

P = 128
ROWS, TABLE_COLS, PICKS, OUT_ROWS = 512, 2048, 512, 512
ROW_BLOCKS = ROWS // P
OUT_BLOCKS = OUT_ROWS // P
EARLY = ROW_BLOCKS // 2
LATE = ROW_BLOCKS - EARLY
PIECES = 2
PIECE = PICKS // PIECES
WARM_UPS = EARLY * OUT_BLOCKS * PIECES

FLOPS = 2 * ROWS * OUT_ROWS * PICKS

F32, BF16, U16 = mybir.dt.float32, mybir.dt.bfloat16, mybir.dt.uint16
SQUARE = mybir.ActivationFunctionType.Square
MULT = mybir.AluOpType.mult


def tile_lookup_gate_sq_none_kernel(tc, tab, y, w, offs, out):
    nc = tc.nc
    tab_rows = tab.rearrange("(p k) s -> p k s", k=ROW_BLOCKS)
    y_rows = y.rearrange("(p k) j -> p k j", k=ROW_BLOCKS)
    w_rows = w.rearrange("(p k) m -> p k m", k=ROW_BLOCKS)

    with (
        tc.tile_pool(name="held", bufs=1) as held,
        tc.psum_pool(name="psum", bufs=1) as psum,
    ):
        offsets = held.tile([P, PICKS // 16], U16, name="offsets")
        windows = [held.tile([P, TABLE_COLS], F32, name=f"window{k}") for k in range(ROW_BLOCKS)]
        squares = [held.tile([P, PICKS], F32, name=f"squares{k}") for k in range(ROW_BLOCKS)]
        gated = [held.tile([P, PICKS], BF16, name=f"gated{k}") for k in range(ROW_BLOCKS)]
        y_early = held.tile([P, EARLY, PICKS], F32, name="y_early")
        y_late = [held.tile([P, LATE, PIECE], F32, name=f"y_late{h}") for h in range(PIECES)]
        w_early = held.tile([P, EARLY, OUT_ROWS], BF16, name="w_early")
        w_late = held.tile([P, LATE, OUT_ROWS], BF16, name="w_late")
        sums = [[psum.tile([P, PIECE], F32, name=f"sums{b}_{h}") for h in range(PIECES)]
                for b in range(OUT_BLOCKS)]
        staged = [[held.tile([P, PIECE], F32, name=f"staged{b}_{h}") for h in range(PIECES)]
                  for b in range(OUT_BLOCKS)]
        pieces = [slice(h * PIECE, (h + 1) * PIECE) for h in range(PIECES)]

        nc.sync.dma_start(windows[0][:], tab_rows[:, 0, :])
        nc.sync.dma_start(offsets[:], offs)
        nc.sync.dma_start(windows[1][:], tab_rows[:, 1, :])
        nc.sync.dma_start(w_early[:], w_rows[:, :EARLY, :])
        nc.sync.dma_start(windows[2][:], tab_rows[:, 2, :])
        nc.sync.dma_start(y_early[:], y_rows[:, :EARLY, :])
        nc.sync.dma_start(windows[3][:], tab_rows[:, 3, :])
        nc.sync.dma_start(y_late[0][:], y_rows[:, EARLY:, pieces[0]])
        nc.sync.dma_start(w_late[:], w_rows[:, EARLY:, :])
        nc.sync.dma_start(y_late[1][:], y_rows[:, EARLY:, pieces[1]])

        weights = [w_early[:, k, :] for k in range(EARLY)]
        weights += [w_late[:, k, :] for k in range(LATE)]

        for n in range(WARM_UPS):
            nc.tensor.matmul(sums[0][0][:], weights[0][:, :P], weights[0][:, :PIECE],
                             start=True, stop=True)

        def look_up(k, h):
            entries = offsets[:, h * PIECE // 16:(h + 1) * PIECE // 16]
            nc.scalar.activation(squares[k][:, pieces[h]], windows[k][:].indirect(entries), SQUARE)

        def gate(k, h, stream):
            nc.vector.tensor_tensor(gated[k][:, pieces[h]], squares[k][:, pieces[h]], stream, MULT)

        def accumulate(k, b, h):
            nc.tensor.matmul(sums[b][h][:], weights[k][:, b * P:(b + 1) * P],
                             gated[k][:, pieces[h]],
                             start=(k == 0), stop=(k == ROW_BLOCKS - 1))

        for k in range(ROW_BLOCKS):
            for h in range(PIECES):
                look_up(k, h)

        for k in range(EARLY):
            for h in range(PIECES):
                gate(k, h, y_early[:, k, pieces[h]])
                for b in range(OUT_BLOCKS):
                    accumulate(k, b, h)

        copies = [nc.scalar.copy, nc.vector.tensor_copy]
        for h in range(PIECES):
            for k in range(EARLY, ROW_BLOCKS):
                gate(k, h, y_late[h][:, k - EARLY, :])
            for b in range(OUT_BLOCKS):
                for k in range(EARLY, ROW_BLOCKS):
                    accumulate(k, b, h)
                copies[h](staged[b][h][:], sums[b][h][:])
                nc.sync.dma_start(out[b * P:(b + 1) * P, pieces[h]], staged[b][h][:])
